import numpy as np
import ml_dtypes


def mxq(x, axis, fmt="e4m3"):
    dtype, down = {"e4m3": (ml_dtypes.float8_e4m3fn, 7), "e5m2": (ml_dtypes.float8_e5m2, 14)}[fmt]
    v = np.moveaxis(np.asarray(x, np.float32).astype(ml_dtypes.bfloat16).astype(np.float64), axis, -1)
    blocks = v.reshape(v.shape[:-1] + (-1, 32))
    amax = np.abs(blocks).max(-1, keepdims=True)
    byte = np.maximum(np.where(amax > 0, np.frexp(amax)[1] - 1 + 127, 0) - down, 1)
    scale = np.exp2(byte - 127.0)
    codes = (blocks / scale).astype(np.float32).astype(dtype).astype(np.float64)
    return np.moveaxis((codes * scale).reshape(v.shape), -1, axis)


WIDE = False


def mx_kscale(k):
    if not WIDE:
        return np.ones(k)
    levels = np.array([10, -10, 5, -5, 0])
    if k % 512:
        return np.exp2(np.random.permutation(np.resize(levels, k // 32))).repeat(32)
    a = np.empty((k // 512, 16))
    for p in range(k // 512):
        a[p, :8] = np.random.permutation(np.resize(levels, 8))
        for g in range(8):
            far = levels[np.abs(levels - a[p, g]) >= 10]
            a[p, g + 8] = far[np.random.randint(len(far))]
    return np.exp2(a.ravel()).repeat(32)


def f64(x):
    return np.asarray(x).astype(np.float64)


def striped(idx):
    return np.tile(idx.reshape(-1, 16).T, (8, 1)).astype(np.uint16)


def unstriped(offs):
    return offs[:16].T.reshape(-1).astype(np.int64)


E2M1 = np.array([0.0, 0.5, 1.0, 1.5, 2.0, 3.0, 4.0, 6.0, -0.0, -0.5, -1.0, -1.5, -2.0, -3.0, -4.0, -6.0])


def pack_weight(w, fmt):
    k, n = w.shape
    w = f64(np.asarray(w, np.float32).astype(ml_dtypes.bfloat16)).reshape(k // 32, 32, n)
    amax = np.abs(w).max(1)
    if fmt == "e4m3":
        byte = np.frexp(amax)[1] - 1 + 127 - 7
    else:
        mant, ex = np.frexp(amax / 6.0)
        byte = np.where(mant > 0.5, ex, ex - 1) + 127
    byte = np.clip(np.where(amax > 0, byte, 1), 1, 254)
    scaled = (w * np.exp2(127.0 - byte)[:, None, :]).reshape(k, n).astype(np.float32)
    by_word = np.ascontiguousarray(scaled.reshape(k // 512, 128, 4, n).transpose(0, 1, 3, 2))
    if fmt == "e4m3":
        words = by_word.astype(ml_dtypes.float8_e4m3fn).view(np.uint8)
    else:
        c = by_word.astype(ml_dtypes.float4_e2m1fn).view(np.uint8) & 0xF
        words = (c[..., 0::2] | (c[..., 1::2] << 4)).reshape(k // 512, 128, 2 * n)
    return np.ascontiguousarray(words), np.ascontiguousarray(byte.astype(np.uint8).reshape(k // 512, 16, n))


def unpack_weight(words, scales, fmt):
    g, _, n = scales.shape
    words = np.ascontiguousarray(words).reshape(g, 128, n, -1)
    if fmt == "e4m3":
        vals = words.view(ml_dtypes.float8_e4m3fn).astype(np.float64)
    else:
        nib = np.empty((g, 128, n, 4), np.uint8)
        nib[..., 0::2] = words & 0xF
        nib[..., 1::2] = words >> 4
        vals = E2M1[nib]
    vals = vals * np.repeat(np.exp2(scales.astype(np.float64) - 127.0), 8, axis=1)[..., None]
    return vals.transpose(0, 1, 3, 2).reshape(g * 512, n)


def pack_table(v):
    words, scales = pack_weight(v, "e4m3")
    return np.concatenate([words.reshape(words.shape[0], -1), scales.reshape(scales.shape[0], -1)], axis=1)


def unpack_table(tab):
    g, t = tab.shape[0], tab.shape[1] // 528
    return unpack_weight(tab[:, :512 * t].reshape(g, 128, t, 4), tab[:, 512 * t:].reshape(g, 16, t), "e4m3")


O, K, M, T, S = 512, 1024, 128, 4096, 1024


def setup_inputs():
    n = np.random.standard_normal
    s = mx_kscale(K)[:, None]
    w = n((K, M)) / np.sqrt(K) / s
    p_w4 = pack_weight(w[O:], "e2m1")
    return {
        "tab": pack_table(n((K, T)) * s),
        "w8": (w[:O]).astype(np.float32),
        "w4_words": p_w4[0],
        "w4_scales": p_w4[1],
        "gate": (n((128, 1024))).astype(np.float32),
        "offs": striped(np.random.permutation(T)[:S]),
    }


def reference(tab, w8, w4_words, w4_scales, gate, offs):
    tab_ = unpack_table(tab)[:, unstriped(offs)]
    w8_ = mxq(f64(w8), 0, "e4m3")
    w4_ = unpack_weight(w4_words, w4_scales, "e2m1")
    y = w8_.T @ tab_[:O] + w4_.T @ tab_[O:]
    return f64(gate) * y

@@ -1,0 +1,115 @@
+from contextlib import ExitStack
+
+import concourse.mybir as mybir
+
+O, K, M, T, S = 512, 1024, 128, 4096, 1024
+FLOPS = 2 * K * M * S
+
+P = 128
+PACK = 4
+HALF = 512
+QUARTER = T // 4
+
+F32 = mybir.dt.float32
+BF16 = mybir.dt.bfloat16
+I32 = mybir.dt.int32
+U32 = mybir.dt.uint32
+U16 = mybir.dt.uint16
+U8 = mybir.dt.uint8
+E4M3X4 = mybir.dt.float8_e4m3fn_x4
+E2M1X4 = mybir.dt.float4_e2m1fn_x4
+MULT = mybir.AluOpType.mult
+
+
+def tile_list_tabo_mul_kernel(tc, tab, w8, w4_words, w4_scales, gate, offs, out):
+    nc = tc.nc
+    with ExitStack() as ctx:
+        keep = ctx.enter_context(tc.tile_pool(name="keep", bufs=1))
+        psum = ctx.enter_context(tc.psum_pool(name="psum", bufs=1))
+
+        offsets = keep.tile([P, S // 16], U16, name="offsets")
+        planes = keep.tile([P, T], U8, name="planes", tag="planes", align_bytes=64)
+        words = keep.tile([P, 2 * T], I32, name="words", align_bytes=64)
+        picked = [keep.tile([P, S], U32, name="picked0", align_bytes=64)]
+        picked_planes = keep.tile([P, S], U8, name="picked_planes", align_bytes=64)
+        w8_raw = keep.tile([P, PACK, M], F32, name="w8_raw", tag="staged")
+        w8_grouped = keep.tile([P, M, PACK], BF16, name="w8_grouped", align_bytes=64)
+        w8_codes = keep.tile([P, M], U32, name="w8_codes", align_bytes=64)
+        w8_plane = keep.tile([P, M], U8, name="w8_plane", align_bytes=64)
+        w4_bytes = keep.tile([P, 3 * M], U8, name="w4_bytes", align_bytes=64)
+        w4_codes, w4_plane = w4_bytes[:, 0 : 2 * M], w4_bytes[:, 2 * M : 3 * M]
+
+        word_rows = [tab[a, 0 : 512 * T].rearrange("(p x) -> p x", p=P) for a in range(2)]
+        scale_rows = [tab[a, 512 * T : 528 * T].rearrange("(q t) -> q t", q=16) for a in range(2)]
+
+        nc.vector.memset(planes[:].bitcast(I32), 0)
+        nc.vector.memset(words[:, QUARTER : 5 * QUARTER : QUARTER], 0)
+        nc.vector.memset(w4_bytes[:].bitcast(I32), 0)
+
+        def load_words(first, last):
+            a, start = divmod(first, 4)
+            stop = start + last - first
+            nc.sync.dma_start(
+                words[:, first * QUARTER : last * QUARTER],
+                word_rows[a][:, 4 * start * QUARTER : 4 * stop * QUARTER].bitcast(I32),
+            )
+
+        def load_scale_rows(first, last):
+            for r, a in [divmod(i, 2) for i in range(first, last)]:
+                row = r + (4 if a == 0 else 0)
+                nc.sync.dma_start(planes[row:P:32, :].bitcast(I32), scale_rows[a][r:16:4, :].bitcast(I32))
+
+        nc.gpsimd.dma_start(w8_raw[:], w8.rearrange("(p j) n -> p j n", j=PACK))
+        nc.gpsimd.dma_start(w4_codes.bitcast(I32), w4_words[0].bitcast(I32))
+        nc.sync.dma_start(offsets[:], offs)
+        load_words(0, 1)
+        load_scale_rows(0, 5)
+        load_words(1, 3)
+        load_scale_rows(5, 8)
+        load_words(3, 4)
+        load_words(4, 8)
+        for q in range(4):
+            nc.sync.dma_start(
+                w4_plane[32 * q : 32 * q + 4, :].bitcast(I32), w4_scales[0, 4 * q : 4 * q + 4, :].bitcast(I32)
+            )
+
+        nc.scalar.copy(out=w8_grouped[:], in_=w8_raw[:].rearrange("p j n -> p n j"))
+        gates = keep.tile([P, S], F32, name="gates", tag="staged")
+        nc.sync.dma_start(gates[:], gate)
+
+        nc.vector.tensor_copy(picked_planes[:], planes[:].indirect(offsets[:]))
+        picked.append(keep.tile([P, S], U32, name="picked1", tag="planes", align_bytes=64))
+        nc.vector.tensor_copy(picked[0][:], words[:, 0:T].bitcast(U32).indirect(offsets[:]))
+        nc.vector.quantize_mx(
+            out=w8_codes[:].bitcast(E4M3X4), scales=w8_plane[:], in_=w8_grouped[:].rearrange("p n j -> p (n j)")
+        )
+        halves = [slice(h * HALF, (h + 1) * HALF) for h in range(2)]
+        banks = [psum.tile([M, HALF], F32, name=f"bank{h}") for h in range(2)]
+        for h in range(2):
+            nc.tensor.matmul_mx(
+                out=banks[h][:],
+                lhsT=w8_codes[:].bitcast(E4M3X4),
+                lhsT_scale=w8_plane[:],
+                rhs=picked[0][:, halves[h]].bitcast(E4M3X4),
+                rhs_scale=picked_planes[4:P, halves[h]],
+                start=True,
+                stop=False,
+            )
+        for h in range(2):
+            nc.vector.tensor_copy(
+                picked[1][:, halves[h]],
+                words[:, T : 2 * T].bitcast(U32).indirect(offsets[:, h * HALF // 16 : (h + 1) * HALF // 16]),
+            )
+            nc.tensor.matmul_mx(
+                out=banks[h][:],
+                lhsT=w4_codes.bitcast(E2M1X4),
+                lhsT_scale=w4_plane,
+                rhs=picked[1][:, halves[h]].bitcast(E4M3X4),
+                rhs_scale=picked_planes[:, halves[h]],
+                start=False,
+                stop=True,
+            )
+        for h in range(2):
+            result = keep.tile([M, HALF], F32, name=f"result{h}")
+            nc.vector.tensor_tensor(result[:], banks[h][:], gates[:, halves[h]], MULT)
+            nc.sync.dma_start(out[:, halves[h]], result[:])

@@ -8,7 +8,6 @@ FLOPS = 2 * K * M * S
 P = 128
 PACK = 4
 HALF = 512
-QUARTER = T // 4
 
 F32 = mybir.dt.float32
 BF16 = mybir.dt.bfloat16
@@ -28,61 +27,49 @@ def tile_list_tabo_mul_kernel(tc, tab, w8, w4_words, w4_scales, gate, offs, out)
         psum = ctx.enter_context(tc.psum_pool(name="psum", bufs=1))
 
         offsets = keep.tile([P, S // 16], U16, name="offsets")
-        planes = keep.tile([P, T], U8, name="planes", tag="planes", align_bytes=64)
-        words = keep.tile([P, 2 * T], I32, name="words", align_bytes=64)
-        picked = [keep.tile([P, S], U32, name="picked0", align_bytes=64)]
-        picked_planes = keep.tile([P, S], U8, name="picked_planes", align_bytes=64)
-        w8_raw = keep.tile([P, PACK, M], F32, name="w8_raw", tag="staged")
+        scale_rows = keep.tile([P, T], U8, name="scale_rows", align_bytes=64)
+        picked_rows = keep.tile([P, S], U8, name="picked_rows", align_bytes=64)
+        planes = keep.tile([P, 2 * S + M], U8, name="planes", align_bytes=64)
+        words = [keep.tile([P, T], I32, name=f"words{a}", align_bytes=64) for a in range(2)]
+        picked = [keep.tile([P, S], U32, name=f"picked{a}", align_bytes=64) for a in range(2)]
+        w8_raw = keep.tile([P, PACK, M], F32, name="w8_raw")
         w8_grouped = keep.tile([P, M, PACK], BF16, name="w8_grouped", align_bytes=64)
         w8_codes = keep.tile([P, M], U32, name="w8_codes", align_bytes=64)
         w8_plane = keep.tile([P, M], U8, name="w8_plane", align_bytes=64)
-        w4_bytes = keep.tile([P, 3 * M], U8, name="w4_bytes", align_bytes=64)
-        w4_codes, w4_plane = w4_bytes[:, 0 : 2 * M], w4_bytes[:, 2 * M : 3 * M]
+        w4_codes = keep.tile([P, 2 * M], U8, name="w4_codes", align_bytes=64)
+        gates = keep.tile([P, S], F32, name="gates")
+        w4_plane = planes[:, 2 * S : 2 * S + M]
 
-        word_rows = [tab[a, 0 : 512 * T].rearrange("(p x) -> p x", p=P) for a in range(2)]
-        scale_rows = [tab[a, 512 * T : 528 * T].rearrange("(q t) -> q t", q=16) for a in range(2)]
+        nc.vector.memset(scale_rows[32:64, :].bitcast(I32), 0)
+        nc.vector.memset(scale_rows[64:P, :].bitcast(I32), 0)
+        nc.gpsimd.memset(planes[:].bitcast(I32), 0)
 
-        nc.vector.memset(planes[:].bitcast(I32), 0)
-        nc.vector.memset(words[:, QUARTER : 5 * QUARTER : QUARTER], 0)
-        nc.vector.memset(w4_bytes[:].bitcast(I32), 0)
-
-        def load_words(first, last):
-            a, start = divmod(first, 4)
-            stop = start + last - first
-            nc.sync.dma_start(
-                words[:, first * QUARTER : last * QUARTER],
-                word_rows[a][:, 4 * start * QUARTER : 4 * stop * QUARTER].bitcast(I32),
-            )
-
-        def load_scale_rows(first, last):
-            for r, a in [divmod(i, 2) for i in range(first, last)]:
-                row = r + (4 if a == 0 else 0)
-                nc.sync.dma_start(planes[row:P:32, :].bitcast(I32), scale_rows[a][r:16:4, :].bitcast(I32))
-
-        nc.gpsimd.dma_start(w8_raw[:], w8.rearrange("(p j) n -> p j n", j=PACK))
-        nc.gpsimd.dma_start(w4_codes.bitcast(I32), w4_words[0].bitcast(I32))
+        nc.sync.dma_start(
+            scale_rows[0:32, :].bitcast(I32),
+            tab[:, 512 * T : 528 * T].rearrange("a (q t) -> q a t", q=16).bitcast(I32),
+        )
         nc.sync.dma_start(offsets[:], offs)
-        load_words(0, 1)
-        load_scale_rows(0, 5)
-        load_words(1, 3)
-        load_scale_rows(5, 8)
-        load_words(3, 4)
-        load_words(4, 8)
+        nc.sync.dma_start(w8_raw[:], w8.rearrange("(p j) n -> p j n", j=PACK))
+        nc.sync.dma_start(w4_codes[:].bitcast(I32), w4_words[0].bitcast(I32))
+        for a in range(2):
+            nc.sync.dma_start(words[a][:], tab[a, 0 : 512 * T].rearrange("(p x) -> p x", p=P).bitcast(I32))
+        nc.sync.dma_start(gates[:], gate)
         for q in range(4):
-            nc.sync.dma_start(
+            nc.gpsimd.dma_start(
                 w4_plane[32 * q : 32 * q + 4, :].bitcast(I32), w4_scales[0, 4 * q : 4 * q + 4, :].bitcast(I32)
             )
 
         nc.scalar.copy(out=w8_grouped[:], in_=w8_raw[:].rearrange("p j n -> p n j"))
-        gates = keep.tile([P, S], F32, name="gates", tag="staged")
-        nc.sync.dma_start(gates[:], gate)
 
-        nc.vector.tensor_copy(picked_planes[:], planes[:].indirect(offsets[:]))
-        picked.append(keep.tile([P, S], U32, name="picked1", tag="planes", align_bytes=64))
-        nc.vector.tensor_copy(picked[0][:], words[:, 0:T].bitcast(U32).indirect(offsets[:]))
+        nc.vector.tensor_copy(picked_rows[:], scale_rows[:].indirect(offsets[:]))
+        for q in range(4):
+            nc.scalar.dma_start(
+                planes[32 * q : 32 * q + 4, 0 : 2 * S].bitcast(I32), picked_rows[8 * q : 8 * q + 8, :].bitcast(I32)
+            )
         nc.vector.quantize_mx(
             out=w8_codes[:].bitcast(E4M3X4), scales=w8_plane[:], in_=w8_grouped[:].rearrange("p n j -> p (n j)")
         )
+        nc.vector.tensor_copy(picked[0][:], words[0][:].bitcast(U32).indirect(offsets[:]))
         halves = [slice(h * HALF, (h + 1) * HALF) for h in range(2)]
         banks = [psum.tile([M, HALF], F32, name=f"bank{h}") for h in range(2)]
         for h in range(2):
@@ -91,21 +78,21 @@ def tile_list_tabo_mul_kernel(tc, tab, w8, w4_words, w4_scales, gate, offs, out)
                 lhsT=w8_codes[:].bitcast(E4M3X4),
                 lhsT_scale=w8_plane[:],
                 rhs=picked[0][:, halves[h]].bitcast(E4M3X4),
-                rhs_scale=picked_planes[4:P, halves[h]],
+                rhs_scale=planes[:, h * HALF : (h + 1) * HALF],
                 start=True,
                 stop=False,
             )
         for h in range(2):
             nc.vector.tensor_copy(
                 picked[1][:, halves[h]],
-                words[:, T : 2 * T].bitcast(U32).indirect(offsets[:, h * HALF // 16 : (h + 1) * HALF // 16]),
+                words[1][:].bitcast(U32).indirect(offsets[:, h * HALF // 16 : (h + 1) * HALF // 16]),
             )
             nc.tensor.matmul_mx(
                 out=banks[h][:],
-                lhsT=w4_codes.bitcast(E2M1X4),
+                lhsT=w4_codes[:].bitcast(E2M1X4),
                 lhsT_scale=w4_plane,
                 rhs=picked[1][:, halves[h]].bitcast(E4M3X4),
-                rhs_scale=picked_planes[:, halves[h]],
+                rhs_scale=planes[:, S + h * HALF : S + (h + 1) * HALF],
                 start=False,
                 stop=True,
             )

@@ -27,9 +27,9 @@ def tile_list_tabo_mul_kernel(tc, tab, w8, w4_words, w4_scales, gate, offs, out)
         psum = ctx.enter_context(tc.psum_pool(name="psum", bufs=1))
 
         offsets = keep.tile([P, S // 16], U16, name="offsets")
-        scale_rows = keep.tile([P, T], U8, name="scale_rows", align_bytes=64)
+        scale_rows = keep.tile([P, T], U8, name="scale_rows", tag="late_gates", align_bytes=64)
         picked_rows = keep.tile([P, S], U8, name="picked_rows", align_bytes=64)
-        planes = keep.tile([P, 2 * S + M], U8, name="planes", align_bytes=64)
+        planes = keep.tile([P, 2 * S], U8, name="planes", align_bytes=64)
         words = [keep.tile([P, T], I32, name=f"words{a}", align_bytes=64) for a in range(2)]
         picked = [keep.tile([P, S], U32, name=f"picked{a}", align_bytes=64) for a in range(2)]
         w8_raw = keep.tile([P, PACK, M], F32, name="w8_raw")
@@ -37,12 +37,12 @@ def tile_list_tabo_mul_kernel(tc, tab, w8, w4_words, w4_scales, gate, offs, out)
         w8_codes = keep.tile([P, M], U32, name="w8_codes", align_bytes=64)
         w8_plane = keep.tile([P, M], U8, name="w8_plane", align_bytes=64)
         w4_codes = keep.tile([P, 2 * M], U8, name="w4_codes", align_bytes=64)
-        gates = keep.tile([P, S], F32, name="gates")
-        w4_plane = planes[:, 2 * S : 2 * S + M]
+        w4_plane = keep.tile([P, M], U8, name="w4_plane", align_bytes=64)
 
         nc.vector.memset(scale_rows[32:64, :].bitcast(I32), 0)
         nc.vector.memset(scale_rows[64:P, :].bitcast(I32), 0)
-        nc.gpsimd.memset(planes[:].bitcast(I32), 0)
+        nc.gpsimd.memset(w4_plane[:].bitcast(I32), 0)
+        nc.vector.memset(planes[:].bitcast(I32), 0)
 
         nc.sync.dma_start(
             scale_rows[0:32, :].bitcast(I32),
@@ -50,10 +50,9 @@ def tile_list_tabo_mul_kernel(tc, tab, w8, w4_words, w4_scales, gate, offs, out)
         )
         nc.sync.dma_start(offsets[:], offs)
         nc.sync.dma_start(w8_raw[:], w8.rearrange("(p j) n -> p j n", j=PACK))
-        nc.sync.dma_start(w4_codes[:].bitcast(I32), w4_words[0].bitcast(I32))
         for a in range(2):
             nc.sync.dma_start(words[a][:], tab[a, 0 : 512 * T].rearrange("(p x) -> p x", p=P).bitcast(I32))
-        nc.sync.dma_start(gates[:], gate)
+        nc.sync.dma_start(w4_codes[:].bitcast(I32), w4_words[0].bitcast(I32))
         for q in range(4):
             nc.gpsimd.dma_start(
                 w4_plane[32 * q : 32 * q + 4, :].bitcast(I32), w4_scales[0, 4 * q : 4 * q + 4, :].bitcast(I32)
@@ -63,40 +62,48 @@ def tile_list_tabo_mul_kernel(tc, tab, w8, w4_words, w4_scales, gate, offs, out)
 
         nc.vector.tensor_copy(picked_rows[:], scale_rows[:].indirect(offsets[:]))
         for q in range(4):
-            nc.scalar.dma_start(
-                planes[32 * q : 32 * q + 4, 0 : 2 * S].bitcast(I32), picked_rows[8 * q : 8 * q + 8, :].bitcast(I32)
+            nc.sync.dma_start(
+                planes[32 * q : 32 * q + 4, :].bitcast(I32), picked_rows[8 * q : 8 * q + 8, :].bitcast(I32)
             )
+        gates = keep.tile([P, S], F32, name="gates", tag="late_gates", align_bytes=64)
+        nc.sync.dma_start(gates[:], gate)
         nc.vector.quantize_mx(
             out=w8_codes[:].bitcast(E4M3X4), scales=w8_plane[:], in_=w8_grouped[:].rearrange("p n j -> p (n j)")
         )
         nc.vector.tensor_copy(picked[0][:], words[0][:].bitcast(U32).indirect(offsets[:]))
-        halves = [slice(h * HALF, (h + 1) * HALF) for h in range(2)]
-        banks = [psum.tile([M, HALF], F32, name=f"bank{h}") for h in range(2)]
-        for h in range(2):
+        spans = [(0, HALF), (HALF, HALF + 256), (HALF + 256, S)]
+        banks = [psum.tile([M, stop - start], F32, name=f"bank{b}") for b, (start, stop) in enumerate(spans)]
+        for bank, (start, stop) in zip(banks, spans):
             nc.tensor.matmul_mx(
-                out=banks[h][:],
+                out=bank[:],
                 lhsT=w8_codes[:].bitcast(E4M3X4),
                 lhsT_scale=w8_plane[:],
-                rhs=picked[0][:, halves[h]].bitcast(E4M3X4),
-                rhs_scale=planes[:, h * HALF : (h + 1) * HALF],
+                rhs=picked[0][:, start:stop].bitcast(E4M3X4),
+                rhs_scale=planes[:, start:stop],
                 start=True,
                 stop=False,
             )
         for h in range(2):
             nc.vector.tensor_copy(
-                picked[1][:, halves[h]],
+                picked[1][:, h * HALF : (h + 1) * HALF],
                 words[1][:].bitcast(U32).indirect(offsets[:, h * HALF // 16 : (h + 1) * HALF // 16]),
             )
-            nc.tensor.matmul_mx(
-                out=banks[h][:],
-                lhsT=w4_codes[:].bitcast(E2M1X4),
-                lhsT_scale=w4_plane,
-                rhs=picked[1][:, halves[h]].bitcast(E4M3X4),
-                rhs_scale=planes[:, S + h * HALF : S + (h + 1) * HALF],
-                start=False,
-                stop=True,
-            )
-        for h in range(2):
-            result = keep.tile([M, HALF], F32, name=f"result{h}")
-            nc.vector.tensor_tensor(result[:], banks[h][:], gates[:, halves[h]], MULT)
-            nc.sync.dma_start(out[:, halves[h]], result[:])
+        for bank, (start, stop) in zip(banks, spans):
+            width = HALF if stop - start == HALF else 128
+            for first in range(start, stop, width):
+                nc.tensor.matmul_mx(
+                    out=bank[:, first - start : first - start + width],
+                    lhsT=w4_codes[:].bitcast(E2M1X4),
+                    lhsT_scale=w4_plane[:],
+                    rhs=picked[1][:, first : first + width].bitcast(E4M3X4),
+                    rhs_scale=planes[:, S + first : S + first + width],
+                    start=False,
+                    stop=(first + width == stop),
+                )
+        for bank, (start, stop) in zip(banks, spans):
+            for first in range(start, stop, 256):
+                result = keep.tile([M, 256], F32, name=f"result{first}")
+                nc.vector.tensor_tensor(
+                    result[:], bank[:, first - start : first - start + 256], gates[:, first : first + 256], MULT
+                )
+                nc.sync.dma_start(out[:, first : first + 256], result[:])

@@ -73,9 +73,16 @@ def tile_list_tabo_mul_kernel(tc, tab, w8, w4_words, w4_scales, gate, offs, out)
         nc.vector.tensor_copy(picked[0][:], words[0][:].bitcast(U32).indirect(offsets[:]))
         spans = [(0, HALF), (HALF, HALF + 256), (HALF + 256, S)]
         banks = [psum.tile([M, stop - start], F32, name=f"bank{b}") for b, (start, stop) in enumerate(spans)]
-        for bank, (start, stop) in zip(banks, spans):
+        for h in range(2):
+            nc.vector.tensor_copy(
+                picked[1][:, h * HALF : (h + 1) * HALF],
+                words[1][:].bitcast(U32).indirect(offsets[:, h * HALF // 16 : (h + 1) * HALF // 16]),
+            )
+
+        def first_pass(b):
+            start, stop = spans[b]
             nc.tensor.matmul_mx(
-                out=bank[:],
+                out=banks[b][:],
                 lhsT=w8_codes[:].bitcast(E4M3X4),
                 lhsT_scale=w8_plane[:],
                 rhs=picked[0][:, start:stop].bitcast(E4M3X4),
@@ -83,16 +90,13 @@ def tile_list_tabo_mul_kernel(tc, tab, w8, w4_words, w4_scales, gate, offs, out)
                 start=True,
                 stop=False,
             )
-        for h in range(2):
-            nc.vector.tensor_copy(
-                picked[1][:, h * HALF : (h + 1) * HALF],
-                words[1][:].bitcast(U32).indirect(offsets[:, h * HALF // 16 : (h + 1) * HALF // 16]),
-            )
-        for bank, (start, stop) in zip(banks, spans):
+
+        def second_pass(b):
+            start, stop = spans[b]
             width = HALF if stop - start == HALF else 128
             for first in range(start, stop, width):
                 nc.tensor.matmul_mx(
-                    out=bank[:, first - start : first - start + width],
+                    out=banks[b][:, first - start : first - start + width],
                     lhsT=w4_codes[:].bitcast(E2M1X4),
                     lhsT_scale=w4_plane[:],
                     rhs=picked[1][:, first : first + width].bitcast(E4M3X4),
@@ -100,6 +104,13 @@ def tile_list_tabo_mul_kernel(tc, tab, w8, w4_words, w4_scales, gate, offs, out)
                     start=False,
                     stop=(first + width == stop),
                 )
+
+        first_pass(0)
+        second_pass(0)
+        first_pass(1)
+        first_pass(2)
+        second_pass(1)
+        second_pass(2)
         for bank, (start, stop) in zip(banks, spans):
             for first in range(start, stop, 256):
                 result = keep.tile([M, 256], F32, name=f"result{first}")

@@ -50,13 +50,20 @@ def tile_list_tabo_mul_kernel(tc, tab, w8, w4_words, w4_scales, gate, offs, out)
         )
         nc.sync.dma_start(offsets[:], offs)
         nc.sync.dma_start(w8_raw[:], w8.rearrange("(p j) n -> p j n", j=PACK))
-        for a in range(2):
-            nc.sync.dma_start(words[a][:], tab[a, 0 : 512 * T].rearrange("(p x) -> p x", p=P).bitcast(I32))
-        nc.sync.dma_start(w4_codes[:].bitcast(I32), w4_words[0].bitcast(I32))
-        for q in range(4):
-            nc.gpsimd.dma_start(
+
+        def load_w4_scales(q):
+            nc.sync.dma_start(
                 w4_plane[32 * q : 32 * q + 4, :].bitcast(I32), w4_scales[0, 4 * q : 4 * q + 4, :].bitcast(I32)
             )
+
+        def load_words(a):
+            nc.sync.dma_start(words[a][:], tab[a, 0 : 512 * T].rearrange("(p x) -> p x", p=P).bitcast(I32))
+
+        load_words(0)
+        for q in range(4):
+            load_w4_scales(q)
+        load_words(1)
+        nc.sync.dma_start(w4_codes[:].bitcast(I32), w4_words[0].bitcast(I32))
 
         nc.scalar.copy(out=w8_grouped[:], in_=w8_raw[:].rearrange("p j n -> p n j"))
 
@@ -106,8 +113,8 @@ def tile_list_tabo_mul_kernel(tc, tab, w8, w4_words, w4_scales, gate, offs, out)
                 )
 
         first_pass(0)
-        second_pass(0)
         first_pass(1)
+        second_pass(0)
         first_pass(2)
         second_pass(1)
         second_pass(2)

@@ -27,16 +27,15 @@ def tile_list_tabo_mul_kernel(tc, tab, w8, w4_words, w4_scales, gate, offs, out)
         psum = ctx.enter_context(tc.psum_pool(name="psum", bufs=1))
 
         offsets = keep.tile([P, S // 16], U16, name="offsets")
-        scale_rows = keep.tile([P, T], U8, name="scale_rows", tag="late_gates", align_bytes=64)
+        scale_rows = keep.tile([P, T], U8, name="scale_rows", tag="then_w4_codes", align_bytes=64)
         picked_rows = keep.tile([P, S], U8, name="picked_rows", align_bytes=64)
         planes = keep.tile([P, 2 * S], U8, name="planes", align_bytes=64)
         words = [keep.tile([P, T], I32, name=f"words{a}", align_bytes=64) for a in range(2)]
         picked = [keep.tile([P, S], U32, name=f"picked{a}", align_bytes=64) for a in range(2)]
         w8_raw = keep.tile([P, PACK, M], F32, name="w8_raw")
-        w8_grouped = keep.tile([P, M, PACK], BF16, name="w8_grouped", align_bytes=64)
+        w8_grouped = keep.tile([P, M, PACK], BF16, name="w8_grouped", tag="then_gates", align_bytes=64)
         w8_codes = keep.tile([P, M], U32, name="w8_codes", align_bytes=64)
         w8_plane = keep.tile([P, M], U8, name="w8_plane", align_bytes=64)
-        w4_codes = keep.tile([P, 2 * M], U8, name="w4_codes", align_bytes=64)
         w4_plane = keep.tile([P, M], U8, name="w4_plane", align_bytes=64)
 
         nc.vector.memset(scale_rows[32:64, :].bitcast(I32), 0)
@@ -63,23 +62,23 @@ def tile_list_tabo_mul_kernel(tc, tab, w8, w4_words, w4_scales, gate, offs, out)
         for q in range(4):
             load_w4_scales(q)
         load_words(1)
-        nc.sync.dma_start(w4_codes[:].bitcast(I32), w4_words[0].bitcast(I32))
 
         nc.scalar.copy(out=w8_grouped[:], in_=w8_raw[:].rearrange("p j n -> p n j"))
 
         nc.vector.tensor_copy(picked_rows[:], scale_rows[:].indirect(offsets[:]))
-        for q in range(4):
+        for q in (0, 2, 1, 3):
             nc.sync.dma_start(
                 planes[32 * q : 32 * q + 4, :].bitcast(I32), picked_rows[8 * q : 8 * q + 8, :].bitcast(I32)
             )
-        gates = keep.tile([P, S], F32, name="gates", tag="late_gates", align_bytes=64)
-        nc.sync.dma_start(gates[:], gate)
+        w4_codes = keep.tile([P, 2 * M], U8, name="w4_codes", tag="then_w4_codes", align_bytes=64)
+        nc.sync.dma_start(w4_codes[:].bitcast(I32), w4_words[0].bitcast(I32))
         nc.vector.quantize_mx(
             out=w8_codes[:].bitcast(E4M3X4), scales=w8_plane[:], in_=w8_grouped[:].rearrange("p n j -> p (n j)")
         )
+        gates = keep.tile([P, S], F32, name="gates", tag="then_gates", align_bytes=64)
+        nc.sync.dma_start(gates[:], gate)
         nc.vector.tensor_copy(picked[0][:], words[0][:].bitcast(U32).indirect(offsets[:]))
-        spans = [(0, HALF), (HALF, HALF + 256), (HALF + 256, S)]
-        banks = [psum.tile([M, stop - start], F32, name=f"bank{b}") for b, (start, stop) in enumerate(spans)]
+        banks = [psum.tile([M, 256], F32, name=f"bank{b}") for b in range(4)]
         for h in range(2):
             nc.vector.tensor_copy(
                 picked[1][:, h * HALF : (h + 1) * HALF],
@@ -87,41 +86,38 @@ def tile_list_tabo_mul_kernel(tc, tab, w8, w4_words, w4_scales, gate, offs, out)
             )
 
         def first_pass(b):
-            start, stop = spans[b]
             nc.tensor.matmul_mx(
                 out=banks[b][:],
                 lhsT=w8_codes[:].bitcast(E4M3X4),
                 lhsT_scale=w8_plane[:],
-                rhs=picked[0][:, start:stop].bitcast(E4M3X4),
-                rhs_scale=planes[:, start:stop],
+                rhs=picked[0][:, 256 * b : 256 * (b + 1)].bitcast(E4M3X4),
+                rhs_scale=planes[:, 256 * b : 256 * (b + 1)],
                 start=True,
                 stop=False,
             )
 
         def second_pass(b):
-            start, stop = spans[b]
-            width = HALF if stop - start == HALF else 128
-            for first in range(start, stop, width):
+            for i in range(2):
+                first = 256 * b + 128 * i
                 nc.tensor.matmul_mx(
-                    out=banks[b][:, first - start : first - start + width],
+                    out=banks[b][:, 128 * i : 128 * (i + 1)],
                     lhsT=w4_codes[:].bitcast(E2M1X4),
                     lhsT_scale=w4_plane[:],
-                    rhs=picked[1][:, first : first + width].bitcast(E4M3X4),
-                    rhs_scale=planes[:, S + first : S + first + width],
+                    rhs=picked[1][:, first : first + 128].bitcast(E4M3X4),
+                    rhs_scale=planes[:, S + first : S + first + 128],
                     start=False,
-                    stop=(first + width == stop),
+                    stop=(i == 1),
                 )
 
         first_pass(0)
         first_pass(1)
         second_pass(0)
-        first_pass(2)
         second_pass(1)
+        first_pass(2)
+        first_pass(3)
         second_pass(2)
-        for bank, (start, stop) in zip(banks, spans):
-            for first in range(start, stop, 256):
-                result = keep.tile([M, 256], F32, name=f"result{first}")
-                nc.vector.tensor_tensor(
-                    result[:], bank[:, first - start : first - start + 256], gates[:, first : first + 256], MULT
-                )
-                nc.sync.dma_start(out[:, first : first + 256], result[:])
+        second_pass(3)
+        for b in range(4):
+            result = keep.tile([M, 256], F32, name=f"result{b}")
+            nc.vector.tensor_tensor(result[:], banks[b][:], gates[:, 256 * b : 256 * (b + 1)], MULT)
+            nc.sync.dma_start(out[:, 256 * b : 256 * (b + 1)], result[:])

@@ -27,20 +27,19 @@ def tile_list_tabo_mul_kernel(tc, tab, w8, w4_words, w4_scales, gate, offs, out)
         psum = ctx.enter_context(tc.psum_pool(name="psum", bufs=1))
 
         offsets = keep.tile([P, S // 16], U16, name="offsets")
-        scale_rows = keep.tile([P, T], U8, name="scale_rows", tag="then_w4_codes", align_bytes=64)
-        picked_rows = keep.tile([P, S], U8, name="picked_rows", align_bytes=64)
-        planes = keep.tile([P, 2 * S], U8, name="planes", align_bytes=64)
+        scale_rows = keep.tile([P, T], U8, name="scale_rows", align_bytes=64)
+        picked_rows = keep.tile([P, S], U8, name="picked_rows", tag="then_w4_codes", align_bytes=64)
+        planes = keep.tile([P, 2 * (S + M)], U8, name="planes", align_bytes=64)
         words = [keep.tile([P, T], I32, name=f"words{a}", align_bytes=64) for a in range(2)]
         picked = [keep.tile([P, S], U32, name=f"picked{a}", align_bytes=64) for a in range(2)]
         w8_raw = keep.tile([P, PACK, M], F32, name="w8_raw")
         w8_grouped = keep.tile([P, M, PACK], BF16, name="w8_grouped", tag="then_gates", align_bytes=64)
         w8_codes = keep.tile([P, M], U32, name="w8_codes", align_bytes=64)
         w8_plane = keep.tile([P, M], U8, name="w8_plane", align_bytes=64)
-        w4_plane = keep.tile([P, M], U8, name="w4_plane", align_bytes=64)
+        carried = keep.tile([32, S + M], U8, name="carried", align_bytes=64)
 
         nc.vector.memset(scale_rows[32:64, :].bitcast(I32), 0)
         nc.vector.memset(scale_rows[64:P, :].bitcast(I32), 0)
-        nc.gpsimd.memset(w4_plane[:].bitcast(I32), 0)
         nc.vector.memset(planes[:].bitcast(I32), 0)
 
         nc.sync.dma_start(
@@ -48,27 +47,25 @@ def tile_list_tabo_mul_kernel(tc, tab, w8, w4_words, w4_scales, gate, offs, out)
             tab[:, 512 * T : 528 * T].rearrange("a (q t) -> q a t", q=16).bitcast(I32),
         )
         nc.sync.dma_start(offsets[:], offs)
+        nc.sync.dma_start(
+            carried[:, S : S + M].bitcast(I32),
+            w4_scales[0].bitcast(I32).unsqueeze(1).to_broadcast([16, 2, M // 4]),
+        )
         nc.sync.dma_start(w8_raw[:], w8.rearrange("(p j) n -> p j n", j=PACK))
-
-        def load_w4_scales(q):
-            nc.sync.dma_start(
-                w4_plane[32 * q : 32 * q + 4, :].bitcast(I32), w4_scales[0, 4 * q : 4 * q + 4, :].bitcast(I32)
-            )
 
         def load_words(a):
             nc.sync.dma_start(words[a][:], tab[a, 0 : 512 * T].rearrange("(p x) -> p x", p=P).bitcast(I32))
 
         load_words(0)
-        for q in range(4):
-            load_w4_scales(q)
         load_words(1)
 
         nc.scalar.copy(out=w8_grouped[:], in_=w8_raw[:].rearrange("p j n -> p n j"))
 
         nc.vector.tensor_copy(picked_rows[:], scale_rows[:].indirect(offsets[:]))
+        nc.vector.tensor_copy(carried[:, 0:S].bitcast(I32), picked_rows[0:32, :].bitcast(I32))
         for q in (0, 2, 1, 3):
             nc.sync.dma_start(
-                planes[32 * q : 32 * q + 4, :].bitcast(I32), picked_rows[8 * q : 8 * q + 8, :].bitcast(I32)
+                planes[32 * q : 32 * q + 4, :].bitcast(I32), carried[8 * q : 8 * q + 8, :].bitcast(I32)
             )
         w4_codes = keep.tile([P, 2 * M], U8, name="w4_codes", tag="then_w4_codes", align_bytes=64)
         nc.sync.dma_start(w4_codes[:].bitcast(I32), w4_words[0].bitcast(I32))
@@ -102,9 +99,9 @@ def tile_list_tabo_mul_kernel(tc, tab, w8, w4_words, w4_scales, gate, offs, out)
                 nc.tensor.matmul_mx(
                     out=banks[b][:, 128 * i : 128 * (i + 1)],
                     lhsT=w4_codes[:].bitcast(E2M1X4),
-                    lhsT_scale=w4_plane[:],
+                    lhsT_scale=planes[:, (b // 2) * (S + M) + S : (b // 2 + 1) * (S + M)],
                     rhs=picked[1][:, first : first + 128].bitcast(E4M3X4),
-                    rhs_scale=planes[:, S + first : S + first + 128],
+                    rhs_scale=planes[:, S + M + first : S + M + first + 128],
                     start=False,
                     stop=(i == 1),
                 )

@@ -28,12 +28,12 @@ def tile_list_tabo_mul_kernel(tc, tab, w8, w4_words, w4_scales, gate, offs, out)
 
         offsets = keep.tile([P, S // 16], U16, name="offsets")
         scale_rows = keep.tile([P, T], U8, name="scale_rows", align_bytes=64)
-        picked_rows = keep.tile([P, S], U8, name="picked_rows", tag="then_w4_codes", align_bytes=64)
+        picked_rows = keep.tile([P, S], U8, name="picked_rows", tag="then_gates", align_bytes=64)
         planes = keep.tile([P, 2 * (S + M)], U8, name="planes", align_bytes=64)
         words = [keep.tile([P, T], I32, name=f"words{a}", align_bytes=64) for a in range(2)]
-        picked = [keep.tile([P, S], U32, name=f"picked{a}", align_bytes=64) for a in range(2)]
+        picked = keep.tile([P, S], U32, name="picked", align_bytes=64)
         w8_raw = keep.tile([P, PACK, M], F32, name="w8_raw")
-        w8_grouped = keep.tile([P, M, PACK], BF16, name="w8_grouped", tag="then_gates", align_bytes=64)
+        w8_grouped = keep.tile([P, M, PACK], BF16, name="w8_grouped", tag="then_last_pick", align_bytes=64)
         w8_codes = keep.tile([P, M], U32, name="w8_codes", align_bytes=64)
         w8_plane = keep.tile([P, M], U8, name="w8_plane", align_bytes=64)
         carried = keep.tile([32, S + M], U8, name="carried", align_bytes=64)
@@ -51,14 +51,16 @@ def tile_list_tabo_mul_kernel(tc, tab, w8, w4_words, w4_scales, gate, offs, out)
             carried[:, S : S + M].bitcast(I32),
             w4_scales[0].bitcast(I32).unsqueeze(1).to_broadcast([16, 2, M // 4]),
         )
-        nc.sync.dma_start(w8_raw[:], w8.rearrange("(p j) n -> p j n", j=PACK))
 
         def load_words(a):
             nc.sync.dma_start(words[a][:], tab[a, 0 : 512 * T].rearrange("(p x) -> p x", p=P).bitcast(I32))
 
         load_words(0)
         load_words(1)
+        nc.sync.dma_start(w8_raw[:], w8.rearrange("(p j) n -> p j n", j=PACK))
 
+        w4_codes = keep.tile([P, 2 * M], U8, name="w4_codes", align_bytes=64)
+        nc.sync.dma_start(w4_codes[:].bitcast(I32), w4_words[0].bitcast(I32))
         nc.scalar.copy(out=w8_grouped[:], in_=w8_raw[:].rearrange("p j n -> p n j"))
 
         nc.vector.tensor_copy(picked_rows[:], scale_rows[:].indirect(offsets[:]))
@@ -67,30 +69,27 @@ def tile_list_tabo_mul_kernel(tc, tab, w8, w4_words, w4_scales, gate, offs, out)
             nc.sync.dma_start(
                 planes[32 * q : 32 * q + 4, :].bitcast(I32), carried[8 * q : 8 * q + 8, :].bitcast(I32)
             )
-        w4_codes = keep.tile([P, 2 * M], U8, name="w4_codes", tag="then_w4_codes", align_bytes=64)
-        nc.sync.dma_start(w4_codes[:].bitcast(I32), w4_words[0].bitcast(I32))
+        gates = keep.tile([P, S], F32, name="gates", tag="then_gates", align_bytes=64)
+        nc.sync.dma_start(gates[:], gate)
+        nc.vector.tensor_copy(picked[:], words[0][:].bitcast(U32).indirect(offsets[:]))
+        banks = [psum.tile([M, 256], F32, name=f"bank{b}") for b in range(4)]
+        late = [keep.tile([P, HALF], U32, name="late0", align_bytes=64)]
+        nc.vector.tensor_copy(late[0][:], words[1][:].bitcast(U32).indirect(offsets[:, 0 : HALF // 16]))
         nc.vector.quantize_mx(
             out=w8_codes[:].bitcast(E4M3X4), scales=w8_plane[:], in_=w8_grouped[:].rearrange("p n j -> p (n j)")
         )
-        gates = keep.tile([P, S], F32, name="gates", tag="then_gates", align_bytes=64)
-        nc.sync.dma_start(gates[:], gate)
-        nc.vector.tensor_copy(picked[0][:], words[0][:].bitcast(U32).indirect(offsets[:]))
-        banks = [psum.tile([M, 256], F32, name=f"bank{b}") for b in range(4)]
-        for h in range(2):
-            nc.vector.tensor_copy(
-                picked[1][:, h * HALF : (h + 1) * HALF],
-                words[1][:].bitcast(U32).indirect(offsets[:, h * HALF // 16 : (h + 1) * HALF // 16]),
-            )
+        late.append(keep.tile([P, HALF], U32, name="late1", tag="then_last_pick", align_bytes=64))
+        nc.vector.tensor_copy(late[1][:], words[1][:].bitcast(U32).indirect(offsets[:, HALF // 16 : S // 16]))
 
         def first_pass(b):
             nc.tensor.matmul_mx(
                 out=banks[b][:],
                 lhsT=w8_codes[:].bitcast(E4M3X4),
                 lhsT_scale=w8_plane[:],
-                rhs=picked[0][:, 256 * b : 256 * (b + 1)].bitcast(E4M3X4),
+                rhs=picked[:, 256 * b : 256 * (b + 1)].bitcast(E4M3X4),
                 rhs_scale=planes[:, 256 * b : 256 * (b + 1)],
-                start=True,
-                stop=False,
+                start=(b >= 2),
+                stop=(b < 2),
             )
 
         def second_pass(b):
@@ -100,16 +99,16 @@ def tile_list_tabo_mul_kernel(tc, tab, w8, w4_words, w4_scales, gate, offs, out)
                     out=banks[b][:, 128 * i : 128 * (i + 1)],
                     lhsT=w4_codes[:].bitcast(E2M1X4),
                     lhsT_scale=planes[:, (b // 2) * (S + M) + S : (b // 2 + 1) * (S + M)],
-                    rhs=picked[1][:, first : first + 128].bitcast(E4M3X4),
+                    rhs=late[b // 2][:, first % HALF : first % HALF + 128].bitcast(E4M3X4),
                     rhs_scale=planes[:, S + M + first : S + M + first + 128],
-                    start=False,
-                    stop=(i == 1),
+                    start=(b < 2 and i == 0),
+                    stop=(b >= 2 and i == 1),
                 )
 
-        first_pass(0)
-        first_pass(1)
         second_pass(0)
         second_pass(1)
+        first_pass(0)
+        first_pass(1)
         first_pass(2)
         first_pass(3)
         second_pass(2)

@@ -32,8 +32,8 @@ def tile_list_tabo_mul_kernel(tc, tab, w8, w4_words, w4_scales, gate, offs, out)
         planes = keep.tile([P, 2 * (S + M)], U8, name="planes", align_bytes=64)
         words = [keep.tile([P, T], I32, name=f"words{a}", align_bytes=64) for a in range(2)]
         picked = keep.tile([P, S], U32, name="picked", align_bytes=64)
-        w8_raw = keep.tile([P, PACK, M], F32, name="w8_raw")
-        w8_grouped = keep.tile([P, M, PACK], BF16, name="w8_grouped", tag="then_last_pick", align_bytes=64)
+        w8_raw = keep.tile([P, PACK, M], F32, name="w8_raw", tag="then_last_pick", align_bytes=64)
+        w8_grouped = keep.tile([P, M, PACK], BF16, name="w8_grouped", align_bytes=64)
         w8_codes = keep.tile([P, M], U32, name="w8_codes", align_bytes=64)
         w8_plane = keep.tile([P, M], U8, name="w8_plane", align_bytes=64)
         carried = keep.tile([32, S + M], U8, name="carried", align_bytes=64)

@@ -19,6 +19,9 @@ E4M3X4 = mybir.dt.float8_e4m3fn_x4
 E2M1X4 = mybir.dt.float4_e2m1fn_x4
 MULT = mybir.AluOpType.mult
 
+EARLY = 768
+PIECES = (128, 128, 128, 128, 256, 128, 128)
+
 
 def tile_list_tabo_mul_kernel(tc, tab, w8, w4_words, w4_scales, gate, offs, out):
     nc = tc.nc
@@ -29,18 +32,20 @@ def tile_list_tabo_mul_kernel(tc, tab, w8, w4_words, w4_scales, gate, offs, out)
         offsets = keep.tile([P, S // 16], U16, name="offsets")
         scale_rows = keep.tile([P, T], U8, name="scale_rows", align_bytes=64)
         picked_rows = keep.tile([P, S], U8, name="picked_rows", tag="then_gates", align_bytes=64)
-        planes = keep.tile([P, 2 * (S + M)], U8, name="planes", align_bytes=64)
+        planes_a = keep.tile([P, 2 * (M + EARLY)], U8, name="planes_a", align_bytes=64)
+        planes_b = keep.tile([P, 2 * (S - EARLY)], U8, name="planes_b", align_bytes=64)
         words = [keep.tile([P, T], I32, name=f"words{a}", align_bytes=64) for a in range(2)]
         picked = keep.tile([P, S], U32, name="picked", align_bytes=64)
         w8_raw = keep.tile([P, PACK, M], F32, name="w8_raw", tag="then_last_pick", align_bytes=64)
         w8_grouped = keep.tile([P, M, PACK], BF16, name="w8_grouped", align_bytes=64)
         w8_codes = keep.tile([P, M], U32, name="w8_codes", align_bytes=64)
         w8_plane = keep.tile([P, M], U8, name="w8_plane", align_bytes=64)
-        carried = keep.tile([32, S + M], U8, name="carried", align_bytes=64)
+        carried = keep.tile([32, M + S], U8, name="carried", align_bytes=64)
 
         nc.vector.memset(scale_rows[32:64, :].bitcast(I32), 0)
         nc.vector.memset(scale_rows[64:P, :].bitcast(I32), 0)
-        nc.vector.memset(planes[:].bitcast(I32), 0)
+        nc.vector.memset(planes_a[:].bitcast(I32), 0)
+        nc.vector.memset(planes_b[:].bitcast(I32), 0)
 
         nc.sync.dma_start(
             scale_rows[0:32, :].bitcast(I32),
@@ -48,15 +53,15 @@ def tile_list_tabo_mul_kernel(tc, tab, w8, w4_words, w4_scales, gate, offs, out)
         )
         nc.sync.dma_start(offsets[:], offs)
         nc.sync.dma_start(
-            carried[:, S : S + M].bitcast(I32),
+            carried[:, 0:M].bitcast(I32),
             w4_scales[0].bitcast(I32).unsqueeze(1).to_broadcast([16, 2, M // 4]),
         )
 
         def load_words(a):
             nc.sync.dma_start(words[a][:], tab[a, 0 : 512 * T].rearrange("(p x) -> p x", p=P).bitcast(I32))
 
-        load_words(0)
         load_words(1)
+        load_words(0)
         nc.sync.dma_start(w8_raw[:], w8.rearrange("(p j) n -> p j n", j=PACK))
 
         w4_codes = keep.tile([P, 2 * M], U8, name="w4_codes", align_bytes=64)
@@ -64,56 +69,76 @@ def tile_list_tabo_mul_kernel(tc, tab, w8, w4_words, w4_scales, gate, offs, out)
         nc.scalar.copy(out=w8_grouped[:], in_=w8_raw[:].rearrange("p j n -> p n j"))
 
         nc.vector.tensor_copy(picked_rows[:], scale_rows[:].indirect(offsets[:]))
-        nc.vector.tensor_copy(carried[:, 0:S].bitcast(I32), picked_rows[0:32, :].bitcast(I32))
+        nc.vector.tensor_copy(carried[:, M : M + S].bitcast(I32), picked_rows[0:32, :].bitcast(I32))
+        gates = keep.tile([P, S], F32, name="gates", tag="then_gates", align_bytes=64)
         for q in (0, 2, 1, 3):
             nc.sync.dma_start(
-                planes[32 * q : 32 * q + 4, :].bitcast(I32), carried[8 * q : 8 * q + 8, :].bitcast(I32)
+                planes_a[32 * q : 32 * q + 4, :].bitcast(I32), carried[8 * q : 8 * q + 8, 0 : M + EARLY].bitcast(I32)
             )
-        gates = keep.tile([P, S], F32, name="gates", tag="then_gates", align_bytes=64)
-        nc.sync.dma_start(gates[:], gate)
-        nc.vector.tensor_copy(picked[:], words[0][:].bitcast(U32).indirect(offsets[:]))
-        banks = [psum.tile([M, 256], F32, name=f"bank{b}") for b in range(4)]
+        nc.sync.dma_start(gates[:, 0:EARLY], gate[:, 0:EARLY])
+        for q in (0, 2, 1, 3):
+            nc.sync.dma_start(
+                planes_b[32 * q : 32 * q + 4, :].bitcast(I32),
+                carried[8 * q : 8 * q + 8, M + EARLY : M + S].bitcast(I32),
+            )
+        nc.sync.dma_start(gates[:, EARLY:S], gate[:, EARLY:S])
+        nc.vector.tensor_copy(picked[:], words[1][:].bitcast(U32).indirect(offsets[:]))
         late = [keep.tile([P, HALF], U32, name="late0", align_bytes=64)]
-        nc.vector.tensor_copy(late[0][:], words[1][:].bitcast(U32).indirect(offsets[:, 0 : HALF // 16]))
+        nc.vector.tensor_copy(late[0][:], words[0][:].bitcast(U32).indirect(offsets[:, 0 : HALF // 16]))
         nc.vector.quantize_mx(
             out=w8_codes[:].bitcast(E4M3X4), scales=w8_plane[:], in_=w8_grouped[:].rearrange("p n j -> p (n j)")
         )
         late.append(keep.tile([P, HALF], U32, name="late1", tag="then_last_pick", align_bytes=64))
-        nc.vector.tensor_copy(late[1][:], words[1][:].bitcast(U32).indirect(offsets[:, HALF // 16 : S // 16]))
+        nc.vector.tensor_copy(late[1][:], words[0][:].bitcast(U32).indirect(offsets[:, HALF // 16 : S // 16]))
 
-        def first_pass(b):
+        def plane(a, first, width):
+            if first < EARLY:
+                at = a * (M + EARLY) + M + first
+                return planes_a[:, at : at + width]
+            at = a * (S - EARLY) + first - EARLY
+            return planes_b[:, at : at + width]
+
+        spans = [(0, 256), (256, 256), (512, 256), (768, 128), (896, 128)]
+        banks = [psum.tile([M, width], F32, name=f"bank{first}") for first, width in spans]
+
+        def w4_passes(b):
+            first, width = spans[b]
+            for i in range(width // 128):
+                at = (first // HALF) * (M + EARLY)
+                nc.tensor.matmul_mx(
+                    out=banks[b][:, 128 * i : 128 * (i + 1)],
+                    lhsT=w4_codes[:].bitcast(E2M1X4),
+                    lhsT_scale=planes_a[:, at : at + M],
+                    rhs=picked[:, first + 128 * i : first + 128 * (i + 1)].bitcast(E4M3X4),
+                    rhs_scale=plane(1, first + 128 * i, 128),
+                    start=(i == 0),
+                    stop=False,
+                )
+
+        def w8_pass(b):
+            first, width = spans[b]
             nc.tensor.matmul_mx(
                 out=banks[b][:],
                 lhsT=w8_codes[:].bitcast(E4M3X4),
                 lhsT_scale=w8_plane[:],
-                rhs=picked[:, 256 * b : 256 * (b + 1)].bitcast(E4M3X4),
-                rhs_scale=planes[:, 256 * b : 256 * (b + 1)],
-                start=(b >= 2),
-                stop=(b < 2),
+                rhs=late[first // HALF][:, first % HALF : first % HALF + width].bitcast(E4M3X4),
+                rhs_scale=plane(0, first, width),
+                start=False,
+                stop=True,
             )
 
-        def second_pass(b):
-            for i in range(2):
-                first = 256 * b + 128 * i
-                nc.tensor.matmul_mx(
-                    out=banks[b][:, 128 * i : 128 * (i + 1)],
-                    lhsT=w4_codes[:].bitcast(E2M1X4),
-                    lhsT_scale=planes[:, (b // 2) * (S + M) + S : (b // 2 + 1) * (S + M)],
-                    rhs=late[b // 2][:, first % HALF : first % HALF + 128].bitcast(E4M3X4),
-                    rhs_scale=planes[:, S + M + first : S + M + first + 128],
-                    start=(b < 2 and i == 0),
-                    stop=(b >= 2 and i == 1),
-                )
-
-        second_pass(0)
-        second_pass(1)
-        first_pass(0)
-        first_pass(1)
-        first_pass(2)
-        first_pass(3)
-        second_pass(2)
-        second_pass(3)
-        for b in range(4):
-            result = keep.tile([M, 256], F32, name=f"result{b}")
-            nc.vector.tensor_tensor(result[:], banks[b][:], gates[:, 256 * b : 256 * (b + 1)], MULT)
-            nc.sync.dma_start(out[:, 256 * b : 256 * (b + 1)], result[:])
+        w4_passes(0)
+        w4_passes(1)
+        w8_pass(0)
+        w8_pass(1)
+        for b in range(2, 5):
+            w4_passes(b)
+            w8_pass(b)
+        first = 0
+        for width in PIECES:
+            b = max(i for i in range(5) if spans[i][0] <= first)
+            at = first - spans[b][0]
+            result = keep.tile([M, width], F32, name=f"result{first}")
+            nc.vector.tensor_tensor(result[:], banks[b][:, at : at + width], gates[:, first : first + width], MULT)
+            nc.sync.dma_start(out[:, first : first + width], result[:])
+            first = first + width

@@ -20,7 +20,7 @@ E2M1X4 = mybir.dt.float4_e2m1fn_x4
 MULT = mybir.AluOpType.mult
 
 EARLY = 768
-PIECES = (128, 128, 128, 128, 256, 128, 128)
+PIECES = (128, 128, 256, 256, 128, 128)
 
 
 def tile_list_tabo_mul_kernel(tc, tab, w8, w4_words, w4_scales, gate, offs, out):
@@ -40,46 +40,51 @@ def tile_list_tabo_mul_kernel(tc, tab, w8, w4_words, w4_scales, gate, offs, out)
         w8_grouped = keep.tile([P, M, PACK], BF16, name="w8_grouped", align_bytes=64)
         w8_codes = keep.tile([P, M], U32, name="w8_codes", align_bytes=64)
         w8_plane = keep.tile([P, M], U8, name="w8_plane", align_bytes=64)
-        carried = keep.tile([32, M + S], U8, name="carried", align_bytes=64)
+        carried = keep.tile([P, M + S], U8, name="carried", align_bytes=64)
 
-        nc.vector.memset(scale_rows[32:64, :].bitcast(I32), 0)
-        nc.vector.memset(scale_rows[64:P, :].bitcast(I32), 0)
+        nc.vector.memset(scale_rows[:].bitcast(I32), 0)
         nc.vector.memset(planes_a[:].bitcast(I32), 0)
         nc.vector.memset(planes_b[:].bitcast(I32), 0)
 
-        nc.sync.dma_start(
-            scale_rows[0:32, :].bitcast(I32),
-            tab[:, 512 * T : 528 * T].rearrange("a (q t) -> q a t", q=16).bitcast(I32),
-        )
         nc.sync.dma_start(offsets[:], offs)
         nc.sync.dma_start(
-            carried[:, 0:M].bitcast(I32),
+            carried[0:P:4, 0:M].bitcast(I32),
             w4_scales[0].bitcast(I32).unsqueeze(1).to_broadcast([16, 2, M // 4]),
         )
 
-        def load_words(a):
-            nc.sync.dma_start(words[a][:], tab[a, 0 : 512 * T].rearrange("(p x) -> p x", p=P).bitcast(I32))
+        def load_words(a, lo, hi):
+            rows = tab[a, 0 : 512 * T].rearrange("(p x) -> p x", p=P).bitcast(I32)
+            nc.sync.dma_start(words[a][:, lo:hi], rows[:, lo:hi])
 
-        load_words(1)
-        load_words(0)
+        load_words(1, 0, T // 2)
+        nc.sync.dma_start(
+            scale_rows[0:P:4, :].bitcast(I32),
+            tab[:, 512 * T : 528 * T].rearrange("a (q t) -> q a t", q=16).bitcast(I32),
+        )
+        load_words(1, T // 2, T)
+        load_words(0, 0, T)
         nc.sync.dma_start(w8_raw[:], w8.rearrange("(p j) n -> p j n", j=PACK))
 
         w4_codes = keep.tile([P, 2 * M], U8, name="w4_codes", align_bytes=64)
         nc.sync.dma_start(w4_codes[:].bitcast(I32), w4_words[0].bitcast(I32))
-        nc.scalar.copy(out=w8_grouped[:], in_=w8_raw[:].rearrange("p j n -> p n j"))
+        nc.scalar.copy(
+            out=w8_grouped[:].rearrange("p (c i) j -> p c j i", i=4),
+            in_=w8_raw[:].rearrange("p j (c i) -> p c j i", i=4),
+        )
 
         nc.vector.tensor_copy(picked_rows[:], scale_rows[:].indirect(offsets[:]))
-        nc.vector.tensor_copy(carried[:, M : M + S].bitcast(I32), picked_rows[0:32, :].bitcast(I32))
+        nc.vector.tensor_copy(carried[:, M : M + S].bitcast(I32), picked_rows[:].bitcast(I32))
         gates = keep.tile([P, S], F32, name="gates", tag="then_gates", align_bytes=64)
         for q in (0, 2, 1, 3):
             nc.sync.dma_start(
-                planes_a[32 * q : 32 * q + 4, :].bitcast(I32), carried[8 * q : 8 * q + 8, 0 : M + EARLY].bitcast(I32)
+                planes_a[32 * q : 32 * q + 4, :].bitcast(I32),
+                carried[32 * q : 32 * q + 32 : 4, 0 : M + EARLY].bitcast(I32),
             )
         nc.sync.dma_start(gates[:, 0:EARLY], gate[:, 0:EARLY])
         for q in (0, 2, 1, 3):
             nc.sync.dma_start(
                 planes_b[32 * q : 32 * q + 4, :].bitcast(I32),
-                carried[8 * q : 8 * q + 8, M + EARLY : M + S].bitcast(I32),
+                carried[32 * q : 32 * q + 32 : 4, M + EARLY : M + S].bitcast(I32),
             )
         nc.sync.dma_start(gates[:, EARLY:S], gate[:, EARLY:S])
         nc.vector.tensor_copy(picked[:], words[1][:].bitcast(U32).indirect(offsets[:]))

@@ -46,17 +46,16 @@ def tile_list_tabo_mul_kernel(tc, tab, w8, w4_words, w4_scales, gate, offs, out)
         nc.vector.memset(planes_a[:].bitcast(I32), 0)
         nc.vector.memset(planes_b[:].bitcast(I32), 0)
 
-        nc.sync.dma_start(offsets[:], offs)
-        nc.sync.dma_start(
-            carried[0:P:4, 0:M].bitcast(I32),
-            w4_scales[0].bitcast(I32).unsqueeze(1).to_broadcast([16, 2, M // 4]),
-        )
-
         def load_words(a, lo, hi):
             rows = tab[a, 0 : 512 * T].rearrange("(p x) -> p x", p=P).bitcast(I32)
             nc.sync.dma_start(words[a][:, lo:hi], rows[:, lo:hi])
 
         load_words(1, 0, T // 2)
+        nc.sync.dma_start(offsets[:], offs)
+        nc.sync.dma_start(
+            carried[0:P:4, 0:M].bitcast(I32),
+            w4_scales[0].bitcast(I32).unsqueeze(1).to_broadcast([16, 2, M // 4]),
+        )
         nc.sync.dma_start(
             scale_rows[0:P:4, :].bitcast(I32),
             tab[:, 512 * T : 528 * T].rearrange("a (q t) -> q a t", q=16).bitcast(I32),

@@ -53,11 +53,11 @@ def tile_list_tabo_mul_kernel(tc, tab, w8, w4_words, w4_scales, gate, offs, out)
         load_words(1, 0, T // 2)
         nc.sync.dma_start(offsets[:], offs)
         nc.sync.dma_start(
-            carried[0:P:4, 0:M].bitcast(I32),
+            carried[32:96:2, 0:M].bitcast(I32),
             w4_scales[0].bitcast(I32).unsqueeze(1).to_broadcast([16, 2, M // 4]),
         )
         nc.sync.dma_start(
-            scale_rows[0:P:4, :].bitcast(I32),
+            scale_rows[32:96:2, :].bitcast(I32),
             tab[:, 512 * T : 528 * T].rearrange("a (q t) -> q a t", q=16).bitcast(I32),
         )
         load_words(1, T // 2, T)
@@ -77,13 +77,13 @@ def tile_list_tabo_mul_kernel(tc, tab, w8, w4_words, w4_scales, gate, offs, out)
         for q in (0, 2, 1, 3):
             nc.sync.dma_start(
                 planes_a[32 * q : 32 * q + 4, :].bitcast(I32),
-                carried[32 * q : 32 * q + 32 : 4, 0 : M + EARLY].bitcast(I32),
+                carried[32 + 16 * q : 48 + 16 * q : 2, 0 : M + EARLY].bitcast(I32),
             )
         nc.sync.dma_start(gates[:, 0:EARLY], gate[:, 0:EARLY])
         for q in (0, 2, 1, 3):
             nc.sync.dma_start(
                 planes_b[32 * q : 32 * q + 4, :].bitcast(I32),
-                carried[32 * q : 32 * q + 32 : 4, M + EARLY : M + S].bitcast(I32),
+                carried[32 + 16 * q : 48 + 16 * q : 2, M + EARLY : M + S].bitcast(I32),
             )
         nc.sync.dma_start(gates[:, EARLY:S], gate[:, EARLY:S])
         nc.vector.tensor_copy(picked[:], words[1][:].bitcast(U32).indirect(offsets[:]))

@@ -18,8 +18,10 @@ U8 = mybir.dt.uint8
 E4M3X4 = mybir.dt.float8_e4m3fn_x4
 E2M1X4 = mybir.dt.float4_e2m1fn_x4
 MULT = mybir.AluOpType.mult
+ADD = mybir.AluOpType.add
 
 EARLY = 768
+SCALAR_COLUMNS = 80
 PIECES = (128, 128, 256, 256, 128, 128)
 
 
@@ -67,8 +69,16 @@ def tile_list_tabo_mul_kernel(tc, tab, w8, w4_words, w4_scales, gate, offs, out)
         w4_codes = keep.tile([P, 2 * M], U8, name="w4_codes", align_bytes=64)
         nc.sync.dma_start(w4_codes[:].bitcast(I32), w4_words[0].bitcast(I32))
         nc.scalar.copy(
-            out=w8_grouped[:].rearrange("p (c i) j -> p c j i", i=4),
-            in_=w8_raw[:].rearrange("p j (c i) -> p c j i", i=4),
+            out=w8_grouped[:, 0:SCALAR_COLUMNS, :].rearrange("p (c i) j -> p c j i", i=4),
+            in_=w8_raw[:, :, 0:SCALAR_COLUMNS].rearrange("p j (c i) -> p c j i", i=4),
+        )
+        nc.gpsimd.tensor_scalar(
+            w8_grouped[:, SCALAR_COLUMNS:M, :],
+            w8_raw[:, :, SCALAR_COLUMNS:M].rearrange("p j n -> p n j"),
+            1.0,
+            0.0,
+            MULT,
+            ADD,
         )
 
         nc.vector.tensor_copy(picked_rows[:], scale_rows[:].indirect(offsets[:]))

@@ -7,7 +7,6 @@ FLOPS = 2 * K * M * S
 
 P = 128
 PACK = 4
-HALF = 512
 
 F32 = mybir.dt.float32
 BF16 = mybir.dt.bfloat16
@@ -20,33 +19,37 @@ E2M1X4 = mybir.dt.float4_e2m1fn_x4
 MULT = mybir.AluOpType.mult
 ADD = mybir.AluOpType.add
 
-EARLY = 768
+FIRST_PICK = 768
 SCALAR_COLUMNS = 80
-PIECES = (128, 128, 256, 256, 128, 128)
+GATE_CUTS = (0, 384, 640, 1024)
+SPANS = ((0, 128), (128, 256), (384, 256), (640, 256), (896, 128))
 
 
 def tile_list_tabo_mul_kernel(tc, tab, w8, w4_words, w4_scales, gate, offs, out):
     nc = tc.nc
     with ExitStack() as ctx:
         keep = ctx.enter_context(tc.tile_pool(name="keep", bufs=1))
+        shared = ctx.enter_context(tc.tile_pool(name="shared", bufs=1))
         psum = ctx.enter_context(tc.psum_pool(name="psum", bufs=1))
 
         offsets = keep.tile([P, S // 16], U16, name="offsets")
         scale_rows = keep.tile([P, T], U8, name="scale_rows", align_bytes=64)
-        picked_rows = keep.tile([P, S], U8, name="picked_rows", tag="then_gates", align_bytes=64)
-        planes_a = keep.tile([P, 2 * (M + EARLY)], U8, name="planes_a", align_bytes=64)
-        planes_b = keep.tile([P, 2 * (S - EARLY)], U8, name="planes_b", align_bytes=64)
+        planes1 = keep.tile([P, M + S], U8, name="planes1", align_bytes=64)
+        planes0 = keep.tile([P, S], U8, name="planes0", align_bytes=64)
         words = [keep.tile([P, T], I32, name=f"words{a}", align_bytes=64) for a in range(2)]
-        picked = keep.tile([P, S], U32, name="picked", align_bytes=64)
-        w8_raw = keep.tile([P, PACK, M], F32, name="w8_raw", tag="then_last_pick", align_bytes=64)
+        picked1 = keep.tile([P, S], U32, name="picked1", align_bytes=64)
+        picked0_first = keep.tile([P, FIRST_PICK], U32, name="picked0_first", align_bytes=64)
         w8_grouped = keep.tile([P, M, PACK], BF16, name="w8_grouped", align_bytes=64)
         w8_codes = keep.tile([P, M], U32, name="w8_codes", align_bytes=64)
         w8_plane = keep.tile([P, M], U8, name="w8_plane", align_bytes=64)
         carried = keep.tile([P, M + S], U8, name="carried", align_bytes=64)
 
+        at = 4 * S - 256
+        picked_rows = shared.tile([P, S], U8, name="picked_rows", offset=at, align_bytes=64)
+
         nc.vector.memset(scale_rows[:].bitcast(I32), 0)
-        nc.vector.memset(planes_a[:].bitcast(I32), 0)
-        nc.vector.memset(planes_b[:].bitcast(I32), 0)
+        nc.vector.memset(planes1[:].bitcast(I32), 0)
+        nc.vector.memset(planes0[:].bitcast(I32), 0)
 
         def load_words(a, lo, hi):
             rows = tab[a, 0 : 512 * T].rearrange("(p x) -> p x", p=P).bitcast(I32)
@@ -54,20 +57,36 @@ def tile_list_tabo_mul_kernel(tc, tab, w8, w4_words, w4_scales, gate, offs, out)
 
         load_words(1, 0, T // 2)
         nc.sync.dma_start(offsets[:], offs)
-        nc.sync.dma_start(
-            carried[32:96:2, 0:M].bitcast(I32),
-            w4_scales[0].bitcast(I32).unsqueeze(1).to_broadcast([16, 2, M // 4]),
-        )
+        nc.sync.dma_start(carried[34:96:4, 0:M].bitcast(I32), w4_scales[0].bitcast(I32))
         nc.sync.dma_start(
             scale_rows[32:96:2, :].bitcast(I32),
             tab[:, 512 * T : 528 * T].rearrange("a (q t) -> q a t", q=16).bitcast(I32),
         )
         load_words(1, T // 2, T)
         load_words(0, 0, T)
-        nc.sync.dma_start(w8_raw[:], w8.rearrange("(p j) n -> p j n", j=PACK))
 
-        w4_codes = keep.tile([P, 2 * M], U8, name="w4_codes", align_bytes=64)
+        nc.vector.tensor_copy(picked_rows[:], scale_rows[:].indirect(offsets[:]))
+        nc.vector.tensor_copy(carried[:, M : M + S].bitcast(I32), picked_rows[:].bitcast(I32))
+
+        gates = shared.tile([P, S], F32, name="gates", offset=0, align_bytes=64)
+        w4_codes = shared.tile([P, 2 * M], U8, name="w4_codes", offset=at + 256, align_bytes=64)
+        w8_raw = shared.tile([P, PACK, M], F32, name="w8_raw", offset=at + 512, align_bytes=64)
+
+        for q in (0, 2, 1, 3):
+            nc.sync.dma_start(
+                planes1[32 * q : 32 * q + 4, :].bitcast(I32),
+                carried[34 + 16 * q : 48 + 16 * q : 4, :].bitcast(I32),
+            )
         nc.sync.dma_start(w4_codes[:].bitcast(I32), w4_words[0].bitcast(I32))
+        nc.sync.dma_start(w8_raw[:], w8.rearrange("(p j) n -> p j n", j=PACK))
+        for q in (0, 2, 1, 3):
+            nc.sync.dma_start(
+                planes0[32 * q + 4 : 32 * q + 8, :].bitcast(I32),
+                carried[32 + 16 * q : 48 + 16 * q : 4, M : M + S].bitcast(I32),
+            )
+        for lo, hi in zip(GATE_CUTS[:-1], GATE_CUTS[1:]):
+            nc.sync.dma_start(gates[:, lo:hi], gate[:, lo:hi])
+
         nc.scalar.copy(
             out=w8_grouped[:, 0:SCALAR_COLUMNS, :].rearrange("p (c i) j -> p c j i", i=4),
             in_=w8_raw[:, :, 0:SCALAR_COLUMNS].rearrange("p j (c i) -> p c j i", i=4),
@@ -81,78 +100,43 @@ def tile_list_tabo_mul_kernel(tc, tab, w8, w4_words, w4_scales, gate, offs, out)
             ADD,
         )
 
-        nc.vector.tensor_copy(picked_rows[:], scale_rows[:].indirect(offsets[:]))
-        nc.vector.tensor_copy(carried[:, M : M + S].bitcast(I32), picked_rows[:].bitcast(I32))
-        gates = keep.tile([P, S], F32, name="gates", tag="then_gates", align_bytes=64)
-        for q in (0, 2, 1, 3):
-            nc.sync.dma_start(
-                planes_a[32 * q : 32 * q + 4, :].bitcast(I32),
-                carried[32 + 16 * q : 48 + 16 * q : 2, 0 : M + EARLY].bitcast(I32),
-            )
-        nc.sync.dma_start(gates[:, 0:EARLY], gate[:, 0:EARLY])
-        for q in (0, 2, 1, 3):
-            nc.sync.dma_start(
-                planes_b[32 * q : 32 * q + 4, :].bitcast(I32),
-                carried[32 + 16 * q : 48 + 16 * q : 2, M + EARLY : M + S].bitcast(I32),
-            )
-        nc.sync.dma_start(gates[:, EARLY:S], gate[:, EARLY:S])
-        nc.vector.tensor_copy(picked[:], words[1][:].bitcast(U32).indirect(offsets[:]))
-        late = [keep.tile([P, HALF], U32, name="late0", align_bytes=64)]
-        nc.vector.tensor_copy(late[0][:], words[0][:].bitcast(U32).indirect(offsets[:, 0 : HALF // 16]))
+        nc.vector.tensor_copy(picked1[:], words[1][:].bitcast(U32).indirect(offsets[:]))
+        nc.vector.tensor_copy(picked0_first[:], words[0][:].bitcast(U32).indirect(offsets[:, 0 : FIRST_PICK // 16]))
         nc.vector.quantize_mx(
             out=w8_codes[:].bitcast(E4M3X4), scales=w8_plane[:], in_=w8_grouped[:].rearrange("p n j -> p (n j)")
         )
-        late.append(keep.tile([P, HALF], U32, name="late1", tag="then_last_pick", align_bytes=64))
-        nc.vector.tensor_copy(late[1][:], words[0][:].bitcast(U32).indirect(offsets[:, HALF // 16 : S // 16]))
+        picked0_last = shared.tile([P, S - FIRST_PICK], U32, name="picked0_last", offset=at + 1024, align_bytes=64)
+        nc.vector.tensor_copy(
+            picked0_last[:], words[0][:].bitcast(U32).indirect(offsets[:, FIRST_PICK // 16 : S // 16])
+        )
 
-        def plane(a, first, width):
-            if first < EARLY:
-                at = a * (M + EARLY) + M + first
-                return planes_a[:, at : at + width]
-            at = a * (S - EARLY) + first - EARLY
-            return planes_b[:, at : at + width]
-
-        spans = [(0, 256), (256, 256), (512, 256), (768, 128), (896, 128)]
-        banks = [psum.tile([M, width], F32, name=f"bank{first}") for first, width in spans]
-
-        def w4_passes(b):
-            first, width = spans[b]
-            for i in range(width // 128):
-                at = (first // HALF) * (M + EARLY)
-                nc.tensor.matmul_mx(
-                    out=banks[b][:, 128 * i : 128 * (i + 1)],
-                    lhsT=w4_codes[:].bitcast(E2M1X4),
-                    lhsT_scale=planes_a[:, at : at + M],
-                    rhs=picked[:, first + 128 * i : first + 128 * (i + 1)].bitcast(E4M3X4),
-                    rhs_scale=plane(1, first + 128 * i, 128),
-                    start=(i == 0),
-                    stop=False,
-                )
-
-        def w8_pass(b):
-            first, width = spans[b]
+        banks = [psum.tile([M, width], F32, name=f"bank{first}") for first, width in SPANS]
+        for bank, (first, width) in zip(banks, SPANS):
             nc.tensor.matmul_mx(
-                out=banks[b][:],
-                lhsT=w8_codes[:].bitcast(E4M3X4),
-                lhsT_scale=w8_plane[:],
-                rhs=late[first // HALF][:, first % HALF : first % HALF + width].bitcast(E4M3X4),
-                rhs_scale=plane(0, first, width),
-                start=False,
-                stop=True,
+                out=bank[:],
+                lhsT=w4_codes[:].bitcast(E2M1X4),
+                lhsT_scale=planes1[:, 0:M],
+                rhs=picked1[:, first : first + width].bitcast(E4M3X4),
+                rhs_scale=planes1[:, M + first : M + first + width],
+                start=True,
+                stop=False,
             )
-
-        w4_passes(0)
-        w4_passes(1)
-        w8_pass(0)
-        w8_pass(1)
-        for b in range(2, 5):
-            w4_passes(b)
-            w8_pass(b)
-        first = 0
-        for width in PIECES:
-            b = max(i for i in range(5) if spans[i][0] <= first)
-            at = first - spans[b][0]
+        for bank, (first, width) in zip(banks, SPANS):
+            cuts = [first, first + width]
+            if first < FIRST_PICK < first + width:
+                cuts = [first, FIRST_PICK, first + width]
+            for lo, hi in zip(cuts[:-1], cuts[1:]):
+                codes = picked0_first[:, lo:hi] if lo < FIRST_PICK else picked0_last[:, lo - FIRST_PICK : hi - FIRST_PICK]
+                nc.tensor.matmul_mx(
+                    out=bank[:, lo - first : hi - first],
+                    lhsT=w8_codes[:].bitcast(E4M3X4),
+                    lhsT_scale=w8_plane[:],
+                    rhs=codes.bitcast(E4M3X4),
+                    rhs_scale=planes0[4:P, lo:hi],
+                    start=False,
+                    stop=(hi == first + width),
+                )
+        for bank, (first, width) in zip(banks, SPANS):
             result = keep.tile([M, width], F32, name=f"result{first}")
-            nc.vector.tensor_tensor(result[:], banks[b][:, at : at + width], gates[:, first : first + width], MULT)
+            nc.vector.tensor_tensor(result[:], bank[:], gates[:, first : first + width], MULT)
             nc.sync.dma_start(out[:, first : first + width], result[:])
-            first = first + width

@@ -72,17 +72,13 @@ def tile_list_tabo_mul_kernel(tc, tab, w8, w4_words, w4_scales, gate, offs, out)
         w4_codes = shared.tile([P, 2 * M], U8, name="w4_codes", offset=at + 256, align_bytes=64)
         w8_raw = shared.tile([P, PACK, M], F32, name="w8_raw", offset=at + 512, align_bytes=64)
 
-        for q in (0, 2, 1, 3):
-            nc.sync.dma_start(
-                planes1[32 * q : 32 * q + 4, :].bitcast(I32),
-                carried[34 + 16 * q : 48 + 16 * q : 4, :].bitcast(I32),
-            )
+        for r in range(4):
+            nc.sync.dma_start(planes1[r:P:32, :].bitcast(I32), carried[34 + 4 * r : 96 : 16, :].bitcast(I32))
         nc.sync.dma_start(w4_codes[:].bitcast(I32), w4_words[0].bitcast(I32))
         nc.sync.dma_start(w8_raw[:], w8.rearrange("(p j) n -> p j n", j=PACK))
-        for q in (0, 2, 1, 3):
+        for r in range(4):
             nc.sync.dma_start(
-                planes0[32 * q + 4 : 32 * q + 8, :].bitcast(I32),
-                carried[32 + 16 * q : 48 + 16 * q : 4, M : M + S].bitcast(I32),
+                planes0[4 + r : P : 32, :].bitcast(I32), carried[32 + 4 * r : 96 : 16, M : M + S].bitcast(I32)
             )
         for lo, hi in zip(GATE_CUTS[:-1], GATE_CUTS[1:]):
             nc.sync.dma_start(gates[:, lo:hi], gate[:, lo:hi])

@@ -38,18 +38,16 @@ def tile_list_tabo_mul_kernel(tc, tab, w8, w4_words, w4_scales, gate, offs, out)
         planes0 = keep.tile([P, S], U8, name="planes0", align_bytes=64)
         words = [keep.tile([P, T], I32, name=f"words{a}", align_bytes=64) for a in range(2)]
         picked1 = keep.tile([P, S], U32, name="picked1", align_bytes=64)
-        picked0_first = keep.tile([P, FIRST_PICK], U32, name="picked0_first", align_bytes=64)
+        picked0 = [keep.tile([P, FIRST_PICK], U32, name="picked0_first", align_bytes=64)]
+        w4_codes = keep.tile([P, 2 * M], U8, name="w4_codes", align_bytes=64)
         w8_grouped = keep.tile([P, M, PACK], BF16, name="w8_grouped", align_bytes=64)
         w8_codes = keep.tile([P, M], U32, name="w8_codes", align_bytes=64)
         w8_plane = keep.tile([P, M], U8, name="w8_plane", align_bytes=64)
-        carried = keep.tile([P, M + S], U8, name="carried", align_bytes=64)
-
-        at = 4 * S - 256
-        picked_rows = shared.tile([P, S], U8, name="picked_rows", offset=at, align_bytes=64)
+        picked_rows = keep.tile([P, S], U8, name="picked_rows", tag="then_gates", align_bytes=64)
+        w8_raw = shared.tile([P, PACK, M], F32, name="w8_raw", offset=0, align_bytes=64)
 
         nc.vector.memset(scale_rows[:].bitcast(I32), 0)
-        nc.vector.memset(planes1[:].bitcast(I32), 0)
-        nc.vector.memset(planes0[:].bitcast(I32), 0)
+        nc.vector.memset(planes1[:, 0:M].bitcast(I32), 0)
 
         def load_words(a, lo, hi):
             rows = tab[a, 0 : 512 * T].rearrange("(p x) -> p x", p=P).bitcast(I32)
@@ -57,31 +55,16 @@ def tile_list_tabo_mul_kernel(tc, tab, w8, w4_words, w4_scales, gate, offs, out)
 
         load_words(1, 0, T // 2)
         nc.sync.dma_start(offsets[:], offs)
-        nc.sync.dma_start(carried[34:96:4, 0:M].bitcast(I32), w4_scales[0].bitcast(I32))
-        nc.sync.dma_start(
-            scale_rows[32:96:2, :].bitcast(I32),
-            tab[:, 512 * T : 528 * T].rearrange("a (q t) -> q a t", q=16).bitcast(I32),
-        )
+        nc.sync.dma_start(w4_codes[:].bitcast(I32), w4_words[0].bitcast(I32))
+        for a in (1, 0):
+            nc.sync.dma_start(
+                scale_rows[4 - 4 * a : P : 8, :].bitcast(I32),
+                tab[a, 512 * T : 528 * T].rearrange("(q t) -> q t", q=16).bitcast(I32),
+            )
+        nc.sync.dma_start(planes1[0:P:8, 0:M].bitcast(I32), w4_scales[0].bitcast(I32))
         load_words(1, T // 2, T)
         load_words(0, 0, T)
-
-        nc.vector.tensor_copy(picked_rows[:], scale_rows[:].indirect(offsets[:]))
-        nc.vector.tensor_copy(carried[:, M : M + S].bitcast(I32), picked_rows[:].bitcast(I32))
-
-        gates = shared.tile([P, S], F32, name="gates", offset=0, align_bytes=64)
-        w4_codes = shared.tile([P, 2 * M], U8, name="w4_codes", offset=at + 256, align_bytes=64)
-        w8_raw = shared.tile([P, PACK, M], F32, name="w8_raw", offset=at + 512, align_bytes=64)
-
-        for r in range(4):
-            nc.sync.dma_start(planes1[r:P:32, :].bitcast(I32), carried[34 + 4 * r : 96 : 16, :].bitcast(I32))
-        nc.sync.dma_start(w4_codes[:].bitcast(I32), w4_words[0].bitcast(I32))
         nc.sync.dma_start(w8_raw[:], w8.rearrange("(p j) n -> p j n", j=PACK))
-        for r in range(4):
-            nc.sync.dma_start(
-                planes0[4 + r : P : 32, :].bitcast(I32), carried[32 + 4 * r : 96 : 16, M : M + S].bitcast(I32)
-            )
-        for lo, hi in zip(GATE_CUTS[:-1], GATE_CUTS[1:]):
-            nc.sync.dma_start(gates[:, lo:hi], gate[:, lo:hi])
 
         nc.scalar.copy(
             out=w8_grouped[:, 0:SCALAR_COLUMNS, :].rearrange("p (c i) j -> p c j i", i=4),
@@ -96,14 +79,27 @@ def tile_list_tabo_mul_kernel(tc, tab, w8, w4_words, w4_scales, gate, offs, out)
             ADD,
         )
 
+        nc.vector.tensor_copy(picked_rows[:], scale_rows[:].indirect(offsets[:]))
+        nc.vector.tensor_copy(planes0[:].bitcast(I32), picked_rows[:].bitcast(I32))
+        nc.vector.tensor_copy(planes1[:, M : M + S].bitcast(I32), picked_rows[:].bitcast(I32))
+        gates = keep.tile([P, S], F32, name="gates", tag="then_gates", align_bytes=64)
+        for r in range(1, 4):
+            nc.sync.dma_start(planes1[r:P:32, :].bitcast(I32), planes1[8 * r : P : 32, :].bitcast(I32))
+        for r in range(1, 4):
+            nc.sync.dma_start(
+                planes0[4 + r : P : 32, :].bitcast(I32), planes1[8 * r + 4 : P : 32, M : M + S].bitcast(I32)
+            )
+        for lo, hi in zip(GATE_CUTS[:-1], GATE_CUTS[1:]):
+            nc.sync.dma_start(gates[:, lo:hi], gate[:, lo:hi])
+
         nc.vector.tensor_copy(picked1[:], words[1][:].bitcast(U32).indirect(offsets[:]))
-        nc.vector.tensor_copy(picked0_first[:], words[0][:].bitcast(U32).indirect(offsets[:, 0 : FIRST_PICK // 16]))
+        nc.vector.tensor_copy(picked0[0][:], words[0][:].bitcast(U32).indirect(offsets[:, 0 : FIRST_PICK // 16]))
         nc.vector.quantize_mx(
             out=w8_codes[:].bitcast(E4M3X4), scales=w8_plane[:], in_=w8_grouped[:].rearrange("p n j -> p (n j)")
         )
-        picked0_last = shared.tile([P, S - FIRST_PICK], U32, name="picked0_last", offset=at + 1024, align_bytes=64)
+        picked0.append(shared.tile([P, S - FIRST_PICK], U32, name="picked0_last", offset=0, align_bytes=64))
         nc.vector.tensor_copy(
-            picked0_last[:], words[0][:].bitcast(U32).indirect(offsets[:, FIRST_PICK // 16 : S // 16])
+            picked0[1][:], words[0][:].bitcast(U32).indirect(offsets[:, FIRST_PICK // 16 : S // 16])
         )
 
         banks = [psum.tile([M, width], F32, name=f"bank{first}") for first, width in SPANS]
@@ -122,12 +118,11 @@ def tile_list_tabo_mul_kernel(tc, tab, w8, w4_words, w4_scales, gate, offs, out)
             if first < FIRST_PICK < first + width:
                 cuts = [first, FIRST_PICK, first + width]
             for lo, hi in zip(cuts[:-1], cuts[1:]):
-                codes = picked0_first[:, lo:hi] if lo < FIRST_PICK else picked0_last[:, lo - FIRST_PICK : hi - FIRST_PICK]
                 nc.tensor.matmul_mx(
                     out=bank[:, lo - first : hi - first],
                     lhsT=w8_codes[:].bitcast(E4M3X4),
                     lhsT_scale=w8_plane[:],
-                    rhs=codes.bitcast(E4M3X4),
+                    rhs=picked0[lo // FIRST_PICK][:, lo % FIRST_PICK : lo % FIRST_PICK + hi - lo].bitcast(E4M3X4),
                     rhs_scale=planes0[4:P, lo:hi],
                     start=False,
                     stop=(hi == first + width),

@@ -17,10 +17,8 @@ U8 = mybir.dt.uint8
 E4M3X4 = mybir.dt.float8_e4m3fn_x4
 E2M1X4 = mybir.dt.float4_e2m1fn_x4
 MULT = mybir.AluOpType.mult
-ADD = mybir.AluOpType.add
 
 FIRST_PICK = 768
-SCALAR_COLUMNS = 80
 GATE_CUTS = (0, 384, 640, 1024)
 SPANS = ((0, 128), (128, 256), (384, 256), (640, 256), (896, 128))
 
@@ -67,16 +65,8 @@ def tile_list_tabo_mul_kernel(tc, tab, w8, w4_words, w4_scales, gate, offs, out)
         nc.sync.dma_start(w8_raw[:], w8.rearrange("(p j) n -> p j n", j=PACK))
 
         nc.scalar.copy(
-            out=w8_grouped[:, 0:SCALAR_COLUMNS, :].rearrange("p (c i) j -> p c j i", i=4),
-            in_=w8_raw[:, :, 0:SCALAR_COLUMNS].rearrange("p j (c i) -> p c j i", i=4),
-        )
-        nc.gpsimd.tensor_scalar(
-            w8_grouped[:, SCALAR_COLUMNS:M, :],
-            w8_raw[:, :, SCALAR_COLUMNS:M].rearrange("p j n -> p n j"),
-            1.0,
-            0.0,
-            MULT,
-            ADD,
+            out=w8_grouped[:].rearrange("p (c i) j -> p c j i", i=4),
+            in_=w8_raw[:].rearrange("p j (c i) -> p c j i", i=4),
         )
 
         nc.vector.tensor_copy(picked_rows[:], scale_rows[:].indirect(offsets[:]))

from contextlib import ExitStack

import concourse.mybir as mybir

O, K, M, T, S = 512, 1024, 128, 4096, 1024
FLOPS = 2 * K * M * S

P = 128
PACK = 4

F32 = mybir.dt.float32
BF16 = mybir.dt.bfloat16
I32 = mybir.dt.int32
U32 = mybir.dt.uint32
U16 = mybir.dt.uint16
U8 = mybir.dt.uint8
E4M3X4 = mybir.dt.float8_e4m3fn_x4
E2M1X4 = mybir.dt.float4_e2m1fn_x4
MULT = mybir.AluOpType.mult

FIRST_PICK = 768
GATE_CUTS = (0, 384, 640, 1024)
SPANS = ((0, 128), (128, 256), (384, 256), (640, 256), (896, 128))


def tile_list_tabo_mul_kernel(tc, tab, w8, w4_words, w4_scales, gate, offs, out):
    nc = tc.nc
    with ExitStack() as ctx:
        keep = ctx.enter_context(tc.tile_pool(name="keep", bufs=1))
        shared = ctx.enter_context(tc.tile_pool(name="shared", bufs=1))
        psum = ctx.enter_context(tc.psum_pool(name="psum", bufs=1))

        offsets = keep.tile([P, S // 16], U16, name="offsets")
        scale_rows = keep.tile([P, T], U8, name="scale_rows", align_bytes=64)
        planes1 = keep.tile([P, M + S], U8, name="planes1", align_bytes=64)
        planes0 = keep.tile([P, S], U8, name="planes0", align_bytes=64)
        words = [keep.tile([P, T], I32, name=f"words{a}", align_bytes=64) for a in range(2)]
        picked1 = keep.tile([P, S], U32, name="picked1", align_bytes=64)
        picked0 = [keep.tile([P, FIRST_PICK], U32, name="picked0_first", align_bytes=64)]
        w4_codes = keep.tile([P, 2 * M], U8, name="w4_codes", align_bytes=64)
        w8_grouped = keep.tile([P, M, PACK], BF16, name="w8_grouped", align_bytes=64)
        w8_codes = keep.tile([P, M], U32, name="w8_codes", align_bytes=64)
        w8_plane = keep.tile([P, M], U8, name="w8_plane", align_bytes=64)
        picked_rows = keep.tile([P, S], U8, name="picked_rows", tag="then_gates", align_bytes=64)
        w8_raw = shared.tile([P, PACK, M], F32, name="w8_raw", offset=0, align_bytes=64)

        nc.vector.memset(scale_rows[:].bitcast(I32), 0)
        nc.vector.memset(planes1[:, 0:M].bitcast(I32), 0)

        def load_words(a, lo, hi):
            rows = tab[a, 0 : 512 * T].rearrange("(p x) -> p x", p=P).bitcast(I32)
            nc.sync.dma_start(words[a][:, lo:hi], rows[:, lo:hi])

        load_words(1, 0, T // 2)
        nc.sync.dma_start(offsets[:], offs)
        nc.sync.dma_start(w4_codes[:].bitcast(I32), w4_words[0].bitcast(I32))
        for a in (1, 0):
            nc.sync.dma_start(
                scale_rows[4 - 4 * a : P : 8, :].bitcast(I32),
                tab[a, 512 * T : 528 * T].rearrange("(q t) -> q t", q=16).bitcast(I32),
            )
        nc.sync.dma_start(planes1[0:P:8, 0:M].bitcast(I32), w4_scales[0].bitcast(I32))
        load_words(1, T // 2, T)
        load_words(0, 0, T)
        nc.sync.dma_start(w8_raw[:], w8.rearrange("(p j) n -> p j n", j=PACK))

        nc.scalar.copy(
            out=w8_grouped[:].rearrange("p (c i) j -> p c j i", i=4),
            in_=w8_raw[:].rearrange("p j (c i) -> p c j i", i=4),
        )

        nc.vector.tensor_copy(picked_rows[:], scale_rows[:].indirect(offsets[:]))
        nc.vector.tensor_copy(planes0[:].bitcast(I32), picked_rows[:].bitcast(I32))
        nc.vector.tensor_copy(planes1[:, M : M + S].bitcast(I32), picked_rows[:].bitcast(I32))
        gates = keep.tile([P, S], F32, name="gates", tag="then_gates", align_bytes=64)
        for r in range(1, 4):
            nc.sync.dma_start(planes1[r:P:32, :].bitcast(I32), planes1[8 * r : P : 32, :].bitcast(I32))
        for r in range(1, 4):
            nc.sync.dma_start(
                planes0[4 + r : P : 32, :].bitcast(I32), planes1[8 * r + 4 : P : 32, M : M + S].bitcast(I32)
            )
        for lo, hi in zip(GATE_CUTS[:-1], GATE_CUTS[1:]):
            nc.sync.dma_start(gates[:, lo:hi], gate[:, lo:hi])

        nc.vector.tensor_copy(picked1[:], words[1][:].bitcast(U32).indirect(offsets[:]))
        nc.vector.tensor_copy(picked0[0][:], words[0][:].bitcast(U32).indirect(offsets[:, 0 : FIRST_PICK // 16]))
        nc.vector.quantize_mx(
            out=w8_codes[:].bitcast(E4M3X4), scales=w8_plane[:], in_=w8_grouped[:].rearrange("p n j -> p (n j)")
        )
        picked0.append(shared.tile([P, S - FIRST_PICK], U32, name="picked0_last", offset=0, align_bytes=64))
        nc.vector.tensor_copy(
            picked0[1][:], words[0][:].bitcast(U32).indirect(offsets[:, FIRST_PICK // 16 : S // 16])
        )

        banks = [psum.tile([M, width], F32, name=f"bank{first}") for first, width in SPANS]
        for bank, (first, width) in zip(banks, SPANS):
            nc.tensor.matmul_mx(
                out=bank[:],
                lhsT=w4_codes[:].bitcast(E2M1X4),
                lhsT_scale=planes1[:, 0:M],
                rhs=picked1[:, first : first + width].bitcast(E4M3X4),
                rhs_scale=planes1[:, M + first : M + first + width],
                start=True,
                stop=False,
            )
        for bank, (first, width) in zip(banks, SPANS):
            cuts = [first, first + width]
            if first < FIRST_PICK < first + width:
                cuts = [first, FIRST_PICK, first + width]
            for lo, hi in zip(cuts[:-1], cuts[1:]):
                nc.tensor.matmul_mx(
                    out=bank[:, lo - first : hi - first],
                    lhsT=w8_codes[:].bitcast(E4M3X4),
                    lhsT_scale=w8_plane[:],
                    rhs=picked0[lo // FIRST_PICK][:, lo % FIRST_PICK : lo % FIRST_PICK + hi - lo].bitcast(E4M3X4),
                    rhs_scale=planes0[4:P, lo:hi],
                    start=False,
                    stop=(hi == first + width),
                )
        for bank, (first, width) in zip(banks, SPANS):
            result = keep.tile([M, width], F32, name=f"result{first}")
            nc.vector.tensor_tensor(result[:], bank[:], gates[:, first : first + width], MULT)
            nc.sync.dma_start(out[:, first : first + width], result[:])
